import numpy as np
import ml_dtypes


def mxq(x, axis, fmt="e4m3"):
    dtype, down = {"e4m3": (ml_dtypes.float8_e4m3fn, 7), "e5m2": (ml_dtypes.float8_e5m2, 14)}[fmt]
    v = np.moveaxis(np.asarray(x, np.float32).astype(ml_dtypes.bfloat16).astype(np.float64), axis, -1)
    blocks = v.reshape(v.shape[:-1] + (-1, 32))
    amax = np.abs(blocks).max(-1, keepdims=True)
    byte = np.maximum(np.where(amax > 0, np.frexp(amax)[1] - 1 + 127, 0) - down, 1)
    scale = np.exp2(byte - 127.0)
    codes = (blocks / scale).astype(np.float32).astype(dtype).astype(np.float64)
    return np.moveaxis((codes * scale).reshape(v.shape), -1, axis)


WIDE = False


def mx_kscale(k):
    if not WIDE:
        return np.ones(k)
    levels = np.array([10, -10, 5, -5, 0])
    if k % 512:
        return np.exp2(np.random.permutation(np.resize(levels, k // 32))).repeat(32)
    a = np.empty((k // 512, 16))
    for p in range(k // 512):
        a[p, :8] = np.random.permutation(np.resize(levels, 8))
        for g in range(8):
            far = levels[np.abs(levels - a[p, g]) >= 10]
            a[p, g + 8] = far[np.random.randint(len(far))]
    return np.exp2(a.ravel()).repeat(32)


def f64(x):
    return np.asarray(x).astype(np.float64)


def striped(idx):
    return np.tile(idx.reshape(-1, 16).T, (8, 1)).astype(np.uint16)


def unstriped(offs):
    return offs[:16].T.reshape(-1).astype(np.int64)


def striped8(idx):
    return np.concatenate([x.reshape(-1, 16).T for x in idx]).astype(np.uint16)


def runs(offs, k):
    lists = np.stack([offs[16 * r : 16 * r + 16].T.reshape(-1) for r in range(8)]).astype(np.int64)
    return lists[np.arange(k) % 512 // 64]


def pack_weight(w):
    k, n = w.shape
    w = f64(np.asarray(w, np.float32).astype(ml_dtypes.bfloat16)).reshape(k // 32, 32, n)
    amax = np.abs(w).max(1)
    byte = np.clip(np.where(amax > 0, np.frexp(amax)[1] - 1 + 127 - 7, 1), 1, 254)
    scaled = (w * np.exp2(127.0 - byte)[:, None, :]).reshape(k, n).astype(np.float32)
    words = np.ascontiguousarray(scaled.reshape(k // 512, 128, 4, n).transpose(0, 1, 3, 2)).astype(ml_dtypes.float8_e4m3fn).view(np.uint8)
    return words, np.ascontiguousarray(byte.astype(np.uint8).reshape(k // 512, 16, n))


def unpack_weight(words, scales):
    g, p, n, _ = words.shape
    vals = np.ascontiguousarray(words).view(ml_dtypes.float8_e4m3fn).astype(np.float64) * np.repeat(np.exp2(scales.astype(np.float64) - 127.0), 8, axis=1)[..., None]
    return vals.transpose(0, 1, 3, 2).reshape(g * 512, n)


E2M1 = np.array([0.0, 0.5, 1.0, 1.5, 2.0, 3.0, 4.0, 6.0, -0.0, -0.5, -1.0, -1.5, -2.0, -3.0, -4.0, -6.0])


def pack_fp4(w):
    k, n = w.shape
    w = f64(np.asarray(w, np.float32).astype(ml_dtypes.bfloat16)).reshape(k // 32, 32, n)
    amax = np.abs(w).max(1)
    mant, ex = np.frexp(amax / 6.0)
    byte = np.clip(np.where(amax > 0, np.where(mant > 0.5, ex, ex - 1) + 127, 1), 1, 254)
    scaled = (w * np.exp2(127.0 - byte)[:, None, :]).reshape(k, n).astype(np.float32)
    c = np.ascontiguousarray(scaled.reshape(k // 512, 128, 4, n).transpose(0, 1, 3, 2)).astype(ml_dtypes.float4_e2m1fn).view(np.uint8) & 0xF
    words = (c[..., 0::2] | (c[..., 1::2] << 4)).reshape(k // 512, 128, 2 * n)
    return np.ascontiguousarray(words), np.ascontiguousarray(byte.astype(np.uint8).reshape(k // 512, 16, n))


def unpack_fp4(words, scales):
    g, _, n = scales.shape
    words = np.ascontiguousarray(words).reshape(g, 128, n, 2)
    nib = np.empty((g, 128, n, 4), np.uint8)
    nib[..., 0::2] = words & 0xF
    nib[..., 1::2] = words >> 4
    vals = E2M1[nib] * np.repeat(np.exp2(scales.astype(np.float64) - 127.0), 8, axis=1)[..., None]
    return vals.transpose(0, 1, 3, 2).reshape(g * 512, n)


def sigmoid(v):
    return 1.0 / (1.0 + np.exp(-np.maximum(v, -700.0)))

def planes(y):
    n, m = y.shape
    v = y.astype(np.float32).astype(ml_dtypes.bfloat16).astype(np.float64).reshape(n // 32, 32, m)
    top = np.abs(v).max(1)
    byte = np.clip(np.where(top > 0, np.frexp(top)[1] - 1 + 127 - 7, 1), 1, 254)
    codes = (v * np.exp2(127.0 - byte)[:, None, :]).reshape(n, m).astype(np.float32).astype(ml_dtypes.float8_e4m3fn).view(np.uint8)
    words = codes.reshape(n // 512, 128, 4, m).transpose(0, 1, 3, 2)
    return np.ascontiguousarray(words), np.ascontiguousarray(byte.astype(np.uint8).reshape(n // 512, 16, m))


K, T, S, V, N, H = 512, 2048, 512, 256, 512, 512


def setup_inputs():
    n = np.random.standard_normal
    s = mx_kscale(K)[:, None]
    u = mx_kscale(S)
    packed_xT = pack_weight(n((K, T)) * s)
    packed_w1 = pack_fp4(n((S, N)) / np.sqrt(S) / u[:, None])
    return {
        "x_words": packed_xT[0],
        "x_scales": packed_xT[1],
        "wa": (n((K, H)) / np.sqrt(K) / s).astype(np.float32),
        "gt": (np.random.uniform(0.5, 1.5, (S, 1)) * u[:, None]).astype(np.float32),
        "w1_words": packed_w1[0],
        "w1_scales": packed_w1[1],
        "offs": striped(np.random.permutation(T)[:S]),
        "order": striped8(np.stack([np.random.permutation(H) for _ in range(8)])),
    }


def reference(x_words, x_scales, wa, gt, w1_words, w1_scales, offs, order):
    xq = unpack_weight(x_words, x_scales)[:, unstriped(offs)]
    y = xq.T @ mxq(f64(wa), 0, "e4m3")
    o = y[np.arange(S)[:, None], runs(order, S)]
    mx = o.reshape(S, V, 2).max(axis=2)
    mn = o.reshape(S, V, 2).min(axis=2)
    z = f64(gt) * (mx * sigmoid(mn))
    out_0 = unpack_fp4(w1_words, w1_scales).T @ mxq(z, 0, "e4m3")
    return (out_0,) + planes(out_0)

from contextlib import ExitStack

import concourse.mybir as mybir

K, T, S, V, N, H = 512, 2048, 512, 256, 512, 512
FLOPS = 2 * K * S * H + 2 * S * N * V

F32 = mybir.dt.float32
BF16 = mybir.dt.bfloat16
I32 = mybir.dt.int32
U32 = mybir.dt.uint32
U16 = mybir.dt.uint16
U8 = mybir.dt.uint8
FP8X4 = mybir.dt.float8_e4m3fn_x4
FP4X4 = mybir.dt.float4_e2m1fn_x4
ALU = mybir.AluOpType
ACT = mybir.ActivationFunctionType

P = 128
PACK = 4
QUADS = 4
WA_COLS = 128
HALF_V = V // 2


def tile_picked_featwin_none_po_kernel(
    tc, x_words, x_scales, wa, gt, w1_words, w1_scales, offs, order, out_0, out_1, out_2
):
    nc = tc.nc
    with ExitStack() as ctx:
        keep = ctx.enter_context(tc.tile_pool(name="keep", bufs=1))
        psum = ctx.enter_context(tc.psum_pool(name="psum", bufs=1))

        def sb(name, shape, dtype, tag=None):
            return keep.tile(shape, dtype, name=name, tag=tag or name, align_bytes=64)

        offs_sb = sb("offs_sb", [P, S // 16], U16)
        order_sb = sb("order_sb", [P, H // 16], U16)
        xw_all = sb("xw_all", [P, T], U32)
        xs_all = sb("xs_all", [P, T], U8)
        gt_sb = sb("gt_sb", [P, PACK], F32)
        w1w_raw = sb("w1w_raw", [P, 2 * N], U8)
        w1s_raw = sb("w1s_raw", [P, N], U8)
        warm_in = sb("warm_in", [P, 1], F32)
        warm_out = sb("warm_out", [P, 1], F32)

        nc.vector.memset(xs_all[:].bitcast(I32), 0)
        nc.vector.memset(w1s_raw[:].bitcast(I32), 0)
        nc.vector.memset(warm_in[:], 0.0)

        wa_rows = wa.rearrange("(p j) h -> p j h", j=PACK)
        wa_raw = [sb("wa_raw%d" % c, [P, PACK, WA_COLS], F32) for c in range(H // WA_COLS)]

        def load_wa(c):
            nc.sync.dma_start(wa_raw[c][:], wa_rows[:, :, c * WA_COLS : (c + 1) * WA_COLS])

        nc.sync.dma_start(offs_sb[:], offs)
        load_wa(0)
        for q in range(QUADS):
            nc.sync.dma_start(xs_all[32 * q : 32 * q + 4, :].bitcast(I32), x_scales[0, 4 * q : 4 * q + 4, :].bitcast(I32))
        nc.sync.dma_start(xw_all[:].bitcast(I32), x_words[0].rearrange("p c r -> p (c r)").bitcast(I32))
        for c in range(1, H // WA_COLS):
            load_wa(c)
        nc.sync.dma_start(order_sb[:], order)
        nc.sync.dma_start(w1w_raw[:].bitcast(I32), w1_words[0].bitcast(I32))
        for q in range(QUADS):
            nc.sync.dma_start(w1s_raw[32 * q : 32 * q + 4, :].bitcast(I32), w1_scales[0, 4 * q : 4 * q + 4, :].bitcast(I32))
        nc.sync.dma_start(gt_sb[:], gt.rearrange("(p t) o -> p (t o)", t=PACK))

        nc.scalar.activation(warm_out[:], warm_in[:], ACT.Sigmoid)

        xs_picked = sb("xs_picked", [P, S], U8)
        xs_dealt = sb("xs_dealt", [P, S], U8)
        xw_dealt = sb("xw_dealt", [P, S], U32)
        nc.vector.tensor_copy(xs_picked[:], xs_all[:].indirect(offs_sb[:]))
        nc.vector.tensor_copy(
            xs_dealt[:].rearrange("p (t m) -> p t m", t=PACK), xs_picked[:].rearrange("p (m t) -> p t m", t=PACK)
        )
        nc.vector.tensor_copy(xw_dealt[:].rearrange("p (t m) -> p m t", t=PACK), xw_all[:].indirect(offs_sb[:]))

        wa_codes = [sb("wa_codes0", [P, 2 * WA_COLS], U32), sb("wa_codes1", [P, 2 * WA_COLS], U32)]
        wa_scales = [sb("wa_scales0", [P, 2 * WA_COLS], U8), sb("wa_scales1", [P, 2 * WA_COLS], U8)]
        for c in range(H // WA_COLS):
            grouped = sb("wa_grouped%d" % c, [P, WA_COLS * PACK], BF16)
            dst = grouped[:].rearrange("p (c i j) -> p c j i", i=4, j=PACK)
            src = wa_raw[c][:].rearrange("p j (c i) -> p c j i", i=4)
            if c in (1, 2):
                nc.scalar.copy(dst, src)
            else:
                nc.vector.tensor_copy(dst, src)
            cols = slice((c % 2) * WA_COLS, (c % 2 + 1) * WA_COLS)
            nc.vector.quantize_mx(wa_codes[c // 2][:, cols].bitcast(FP8X4), wa_scales[c // 2][:, cols], grouped[:])

        y = [sb("y%d" % t, [P, H], F32) for t in range(PACK)]
        early = [psum.tile([P, 2, 256], F32, name="early%d" % u, tag="bank%d" % u) for u in range(2)]
        late = [psum.tile([P, 256], F32, name="late%d" % t, tag="bank%d" % (2 + t)) for t in range(PACK)]

        def first_product(out, t, codes, scales):
            cols = slice(t * P, (t + 1) * P)
            nc.tensor.matmul_mx(
                out, lhsT=xw_dealt[:, cols].bitcast(FP8X4), lhsT_scale=xs_dealt[:, cols],
                rhs=codes.bitcast(FP8X4), rhs_scale=scales, start=True, stop=True,
            )

        for t in range(PACK):
            first_product(early[t // 2][:, t % 2, :], t, wa_codes[0][:], wa_scales[0][:])
        for c in range(2):
            cols = slice(c * WA_COLS, (c + 1) * WA_COLS)
            for t in range(PACK):
                first_product(late[t][:, cols], t, wa_codes[1][:, cols], wa_scales[1][:, cols])
        for t in range(PACK):
            nc.scalar.copy(y[t][:, 0:256], early[t // 2][:, t % 2, :])
            nc.scalar.copy(y[t][:, 256:512], late[t][:])

        w1w = sb("w1w", [P, 2 * N], U8, tag="wa_grouped3")
        w1s = sb("w1s", [P, N], U8, tag="wa_raw3")
        nc.vector.tensor_copy(
            w1w[:].rearrange("p (t m b) -> p t m b", t=PACK, b=2), w1w_raw[:].rearrange("p (m t b) -> p t m b", t=PACK, b=2)
        )
        nc.vector.tensor_copy(w1s[:].rearrange("p (t m) -> p t m", t=PACK), w1s_raw[:].rearrange("p (m t) -> p t m", t=PACK))

        out_codes = sb("out_codes", [P, V], U32)
        out_scales = sb("out_scales", [P, V], U8)
        out_rows = out_0.rearrange("(p t) v -> p t v", t=PACK)
        out_words = out_1[0].rearrange("p c r -> p (c r)").bitcast(I32)

        def compete(h):
            big = sb("big%d" % h, [P, PACK, HALF_V], F32)
            small = sb("small%d" % h, [P, PACK, HALF_V], F32)
            weighted = sb("weighted%d" % h, [P, PACK, HALF_V], F32)
            gate = sb("gate%d" % h, [P, PACK, HALF_V], F32)
            entries = order_sb[:, h * 16 : (h + 1) * 16]
            for u in range(2):
                lined = sb("lined%d_%d" % (h, u), [P, 2, 2 * HALF_V], F32)
                for e in range(2):
                    nc.vector.tensor_copy(lined[:, e, :], y[2 * u + e][:].indirect(entries))
                pairs = lined[:].rearrange("p e (v s) -> p e v s", s=2)
                ts = slice(2 * u, 2 * u + 2)
                nc.vector.tensor_tensor(big[:, ts, :], pairs[:, :, :, 0], pairs[:, :, :, 1], ALU.max)
                nc.vector.tensor_tensor(small[:, ts, :], pairs[:, :, :, 0], pairs[:, :, :, 1], ALU.min)
                for t in range(2 * u, 2 * u + 2):
                    nc.scalar.activation(weighted[:, t, :], big[:, t, :], ACT.Copy, scale=gt_sb[:, t : t + 1])
                nc.scalar.activation(gate[:, ts, :], small[:, ts, :], ACT.Sigmoid)
            return weighted, gate

        def weigh(h, weighted, gate):
            z = sb("z%d" % h, [P, HALF_V * PACK], BF16)
            nc.vector.tensor_tensor(
                z[:].rearrange("p (c i t) -> p c t i", i=4, t=PACK),
                weighted[:].rearrange("p t (c i) -> p c t i", i=4),
                gate[:].rearrange("p t (c i) -> p c t i", i=4),
                ALU.mult,
            )
            return z

        def mix(h, z):
            z_codes = sb("z_codes%d" % h, [P, HALF_V], U32)
            z_scales = sb("z_scales%d" % h, [P, HALF_V], U8)
            nc.vector.quantize_mx(z_codes[:].bitcast(FP8X4), z_scales[:], z[:])
            result = sb("result%d" % h, [P, PACK, HALF_V], F32)
            for u in range(2):
                bank = psum.tile([P, 2, HALF_V], F32, name="mixed%d_%d" % (h, u), tag="bank%d" % ((6 + 2 * h + u) % 8))
                for e in range(2):
                    t = 2 * u + e
                    nc.tensor.matmul_mx(
                        bank[:, e, :],
                        lhsT=w1w[:, t * 2 * P : (t + 1) * 2 * P].bitcast(FP4X4), lhsT_scale=w1s[:, t * P : (t + 1) * P],
                        rhs=z_codes[:].bitcast(FP8X4), rhs_scale=z_scales[:], start=True, stop=True,
                    )
                nc.scalar.copy(result[:, 2 * u : 2 * u + 2, :], bank[:])
            return result

        def hand_out(h, result):
            cols = slice(h * HALF_V, (h + 1) * HALF_V)
            nc.scalar.dma_start(out_rows[:, :, cols], result[:])
            rounded = sb("rounded%d" % h, [P, HALF_V * PACK], BF16)
            nc.vector.tensor_copy(
                rounded[:].rearrange("p (c i t) -> p c t i", i=4, t=PACK), result[:].rearrange("p t (c i) -> p c t i", i=4)
            )
            nc.vector.quantize_mx(out_codes[:, cols].bitcast(FP8X4), out_scales[:, cols], rounded[:])
            nc.sync.dma_start(out_words[:, cols], out_codes[:, cols].bitcast(I32))

        first = compete(0)
        second = compete(1)
        first_z = weigh(0, *first)
        second_z = weigh(1, *second)
        first_result = mix(0, first_z)
        second_result = mix(1, second_z)
        hand_out(0, first_result)
        hand_out(1, second_result)
        for q in range(QUADS):
            queue = nc.sync if q % 2 == 0 else nc.scalar
            queue.dma_start(out_2[0, 4 * q : 4 * q + 4, :].bitcast(I32), out_scales[32 * q : 32 * q + 4, :].bitcast(I32))
